import numpy as np
CORES = [3,1,0,2]
N = 4
ROOT = 0
def setup_inputs(rng):
    return {"x": rng.standard_normal((N, 128, 256), dtype=np.float32)}
def reference(x):
    y = np.full(x.shape, np.nan, x.dtype)
    y[ROOT] = x.max(axis=0)
    return {"y": y}

@@ -1,0 +1,51 @@
+from concourse.bass import DstId, RemoteDMATransfer
+
+SCRATCH = {
+    "xs": ("sbuf", [128, 256], "float32"),
+    "in0": ("sbuf", [128, 256], "float32"),
+    "in1": ("sbuf", [128, 256], "float32"),
+    "in2": ("sbuf", [128, 256], "float32"),
+    "res": ("sbuf", [128, 256], "float32"),
+}
+SEMAPHORES = ["loaded", "sent", "arrived", "stored"]
+
+ENGINES = 16
+MAX = 2
+
+
+def rank_program(g, core, T, topo):
+    rank = T.rank_of(core)
+    if rank is None:
+        return
+    root = T.cores[0]
+    folder = T.cores[1]
+    senders = [c for c in T.cores if c != folder]
+
+    g.dma_start(T.xs[:], T.x[:]).then_inc(T.sem.loaded, 16)
+    g.wait_ge(T.sem.loaded, 16)
+
+    if core != folder:
+        slot = [T.in0, T.in1, T.in2][senders.index(core)]
+        rid, pid = topo.addr(folder)[:2]
+        g.remote_dma(slot[:], T.xs[:], T.sem.arrived, T.sem.sent, pid, rid, topo.mask(core, folder))
+        g.wait_ge(T.sem.sent, ENGINES)
+    else:
+        g.wait_ge(T.sem.arrived, ENGINES * len(senders))
+        rid, pid = topo.addr(root)[:2]
+        g.remote_dma_fused(
+            [RemoteDMATransfer(
+                dst_ids=[DstId(rid=rid, pnc=pid)],
+                dma_engine_mask=topo.mask(core, root),
+                remote_sem=T.sem.arrived,
+                srcs=[T.xs[:], T.in0[:], T.in1[:], T.in2[:]],
+                dsts=[T.res[:]],
+                alu_op=MAX,
+            )],
+            local_sem=T.sem.sent,
+        )
+        g.wait_ge(T.sem.sent, ENGINES)
+
+    if core == root:
+        g.wait_ge(T.sem.arrived, ENGINES)
+        g.dma_start(T.y[:], T.res[:]).then_inc(T.sem.stored, 16)
+        g.wait_ge(T.sem.stored, 16)

@@ -1,11 +1,17 @@
 from concourse.bass import DstId, RemoteDMATransfer
 
+ROWS = [0, 43, 86, 128]
+W, N = 86, 84
+
 SCRATCH = {
-    "xs": ("sbuf", [128, 256], "float32"),
-    "in0": ("sbuf", [128, 256], "float32"),
-    "in1": ("sbuf", [128, 256], "float32"),
-    "in2": ("sbuf", [128, 256], "float32"),
-    "res": ("sbuf", [128, 256], "float32"),
+    "xs0": ("dram", [128, W], "float32"),
+    "xs1": ("dram", [128, W], "float32"),
+    "xs2": ("dram", [128, N], "float32"),
+    "landw": ("dram", [3, 128, W], "float32"),
+    "landn": ("dram", [3, 128, N], "float32"),
+    "res0": ("dram", [128, W], "float32"),
+    "res1": ("dram", [128, W], "float32"),
+    "res2": ("dram", [128, N], "float32"),
 }
 SEMAPHORES = ["loaded", "sent", "arrived", "stored"]
 
@@ -14,38 +20,47 @@ MAX = 2
 
 
 def rank_program(g, core, T, topo):
-    rank = T.rank_of(core)
-    if rank is None:
+    if T.rank_of(core) is None:
         return
     root = T.cores[0]
-    folder = T.cores[1]
-    senders = [c for c in T.cores if c != folder]
+    folders = [c for c in T.cores if c != root]
+    xs = [T.xs0, T.xs1, T.xs2]
+    res = [T.res0, T.res1, T.res2]
+    land = [T.landw, T.landw, T.landn]
 
-    g.dma_start(T.xs[:], T.x[:]).then_inc(T.sem.loaded, 16)
-    g.wait_ge(T.sem.loaded, 16)
+    for k in range(3):
+        g.dma_start(xs[k][:], T.x[ROWS[k]:ROWS[k + 1], :]).then_inc(T.sem.loaded, 16)
+    g.wait_ge(T.sem.loaded, 48)
 
-    if core != folder:
-        slot = [T.in0, T.in1, T.in2][senders.index(core)]
-        rid, pid = topo.addr(folder)[:2]
-        g.remote_dma(slot[:], T.xs[:], T.sem.arrived, T.sem.sent, pid, rid, topo.mask(core, folder))
-        g.wait_ge(T.sem.sent, ENGINES)
-    else:
-        g.wait_ge(T.sem.arrived, ENGINES * len(senders))
+    calls = 0
+    for k, f in enumerate(folders):
+        if f == core:
+            continue
+        s = [c for c in T.cores if c != f].index(core)
+        rid, pid = topo.addr(f)[:2]
+        g.remote_dma(land[k][s], xs[k][:], T.sem.arrived, T.sem.sent, pid, rid, topo.mask(core, f))
+        calls += 1
+
+    if core != root:
+        k = folders.index(core)
+        g.wait_ge(T.sem.arrived, ENGINES * 3)
         rid, pid = topo.addr(root)[:2]
         g.remote_dma_fused(
             [RemoteDMATransfer(
                 dst_ids=[DstId(rid=rid, pnc=pid)],
                 dma_engine_mask=topo.mask(core, root),
                 remote_sem=T.sem.arrived,
-                srcs=[T.xs[:], T.in0[:], T.in1[:], T.in2[:]],
-                dsts=[T.res[:]],
+                srcs=[xs[k][:], land[k][0], land[k][1], land[k][2]],
+                dsts=[res[k][:]],
                 alu_op=MAX,
             )],
             local_sem=T.sem.sent,
         )
-        g.wait_ge(T.sem.sent, ENGINES)
+        calls += 1
+    else:
+        g.wait_ge(T.sem.arrived, ENGINES * 3)
+        for k in range(3):
+            g.dma_start(T.y[ROWS[k]:ROWS[k + 1], :], res[k][:]).then_inc(T.sem.stored, 16)
+        g.wait_ge(T.sem.stored, 48)
 
-    if core == root:
-        g.wait_ge(T.sem.arrived, ENGINES)
-        g.dma_start(T.y[:], T.res[:]).then_inc(T.sem.stored, 16)
-        g.wait_ge(T.sem.stored, 16)
+    g.wait_ge(T.sem.sent, ENGINES * calls)

from concourse.bass import DstId, RemoteDMATransfer

ROWS = [0, 43, 86, 128]
W, N = 86, 84

SCRATCH = {
    "xs0": ("dram", [128, W], "float32"),
    "xs1": ("dram", [128, W], "float32"),
    "xs2": ("dram", [128, N], "float32"),
    "landw": ("dram", [3, 128, W], "float32"),
    "landn": ("dram", [3, 128, N], "float32"),
    "res0": ("dram", [128, W], "float32"),
    "res1": ("dram", [128, W], "float32"),
    "res2": ("dram", [128, N], "float32"),
}
SEMAPHORES = ["loaded", "sent", "arrived", "stored"]

ENGINES = 16
MAX = 2


def rank_program(g, core, T, topo):
    if T.rank_of(core) is None:
        return
    root = T.cores[0]
    folders = [c for c in T.cores if c != root]
    xs = [T.xs0, T.xs1, T.xs2]
    res = [T.res0, T.res1, T.res2]
    land = [T.landw, T.landw, T.landn]

    for k in range(3):
        g.dma_start(xs[k][:], T.x[ROWS[k]:ROWS[k + 1], :]).then_inc(T.sem.loaded, 16)
    g.wait_ge(T.sem.loaded, 48)

    calls = 0
    for k, f in enumerate(folders):
        if f == core:
            continue
        s = [c for c in T.cores if c != f].index(core)
        rid, pid = topo.addr(f)[:2]
        g.remote_dma(land[k][s], xs[k][:], T.sem.arrived, T.sem.sent, pid, rid, topo.mask(core, f))
        calls += 1

    if core != root:
        k = folders.index(core)
        g.wait_ge(T.sem.arrived, ENGINES * 3)
        rid, pid = topo.addr(root)[:2]
        g.remote_dma_fused(
            [RemoteDMATransfer(
                dst_ids=[DstId(rid=rid, pnc=pid)],
                dma_engine_mask=topo.mask(core, root),
                remote_sem=T.sem.arrived,
                srcs=[xs[k][:], land[k][0], land[k][1], land[k][2]],
                dsts=[res[k][:]],
                alu_op=MAX,
            )],
            local_sem=T.sem.sent,
        )
        calls += 1
    else:
        g.wait_ge(T.sem.arrived, ENGINES * 3)
        for k in range(3):
            g.dma_start(T.y[ROWS[k]:ROWS[k + 1], :], res[k][:]).then_inc(T.sem.stored, 16)
        g.wait_ge(T.sem.stored, 48)

    g.wait_ge(T.sem.sent, ENGINES * calls)
